import numpy as np, ml_dtypes
CORES = [10,34,74,98]
N = 4
BF = ml_dtypes.bfloat16
def gentries(a):
    return np.ascontiguousarray(a.reshape(8, 16, -1).transpose(0, 2, 1)).reshape(8, -1)
def gtable(e):
    e = np.asarray(e); return np.ascontiguousarray(e.reshape(8, -1, 16).transpose(0, 2, 1)).reshape(128, -1).astype(np.int32)
def f(rng, *shape):
    return (rng.standard_normal(shape, dtype=np.float32) * np.exp2(rng.integers(-2, 3, shape[:-1] + (1,)))).astype(BF)
def wide(rng, *shape):
    v = f(rng, *shape).astype(np.float32); k = shape[:-2] + (1, shape[-1])
    return (v * np.exp2(rng.integers(-6, 7, k)) * (rng.random(k) > 0.0625)).astype(BF)
P, E, M, G = 3072, 4096, 256, 256
Z = P + (N - 1) * G
DX, DY = (-1, 0, 1, -1, 1, -1, 0, 1), (-1, -1, -1, 0, 0, 1, 1, 1)
FAR = [[(d, s) for d in range(8) for s in range(4) if max(abs(2 * DX[d] + s % 2 - c % 2), abs(2 * DY[d] + s // 2 - c // 2)) > 1] for c in range(4)]
def kids(rng):
    return rng.permuted(np.tile(np.minimum(np.arange(4 * P), E), (N, 8, 1)), axis=2).reshape(N, 8, 4, P)
def nears(rng, own, ghost):
    u = rng.random((N, 8, 8, M))
    return np.where(u < own, rng.integers(0, P, u.shape), np.where(u < own + ghost, rng.integers(P, Z, u.shape), Z))
def gives(rng):
    return rng.integers(0, P, (N, 8, N - 1, G))
def pack(rng, ki, ne, gi):
    return {"ex": f(rng, N, 128, E), "kid": ki.reshape(N, 8, 4 * P).astype(np.int32), "near": np.stack([gtable(a.reshape(8, 8 * M)) for a in ne]),
            "give": np.stack([gtable(a.reshape(8, (N - 1) * G)) for a in gi]), "tr": f(rng, N, 128, 108)}
def setup_inputs(rng):
    return pack(rng, kids(rng), nears(rng, 0.5, 0.42), gives(rng))
def setup_inputs_ghosts(rng):
    ne = nears(rng, 0.0, 2.0); q = rng.integers(0, N); ne[q] = P + G * rng.integers(0, N - 1) + rng.integers(0, G, (8, 8, M))
    for b in range(N - 1):
        ne[:, :, b, 0] = P + G * b; ne[:, :, b, M - 1] = P + G * b + G - 1
    return pack(rng, kids(rng), ne, gives(rng))
def setup_inputs_empty(rng):
    ne = nears(rng, 0.15, 0.15); ne[:, :, :, ::4] = Z; ne[:, rng.choice(np.array([0, 3, 4, 6, 7]))] = Z
    ki = kids(rng); ki[:, :, :, rng.random(P) < 0.5] = E; b = rng.integers(0, P)
    ki[:, :, :, b] = rng.integers(0, E, (N, 8, 4)); ne[:, 1:3, 0, 1] = b
    ne[:, 5, 7, 2] = b
    return pack(rng, ki, ne, gives(rng))
def setup_inputs_ends(rng):
    ne = rng.choice(np.array([0, P - 1, P, P + G - 1, Z - G, Z - 1, Z]), (N, 8, 8, M)); ki = kids(rng)
    for p in (0, P - 1): ki[:, :, :, p] = rng.permuted(np.tile(np.array([0, E - 1, E, E - 1]), (N, 8, 1)), axis=2)
    return pack(rng, ki, ne, rng.choice(np.array([0, P - 1]), (N, 8, N - 1, G)))
def setup_inputs_alike(rng):
    ne = np.tile(rng.integers(0, Z, (N, 8, 8, 1)), (1, 1, 1, M)); gi = np.tile(rng.integers(0, P, (N, 8, N - 1, 1)), (1, 1, 1, G))
    return pack(rng, rng.integers(0, E, (N, 8, 4, P)), ne, gi)
def setup_inputs_spread(rng):
    d = setup_inputs(rng); d["ex"] = wide(rng, N, 128, E); return d
def check_inputs(d):
    bad = []
    for a, top in (("kid", E), ("near", Z), ("give", P - 1)):
        if d[a].min() < 0 or d[a].max() > top: bad.append(a)
    for a in ("ex", "tr"):
        if not np.isfinite(d[a].astype(np.float32)).all(): bad.append(a)
    return bad
def reference(ex, kid, near, give, tr):
    x = np.concatenate([ex.astype(np.float64).reshape(N, 8, 16, E), np.zeros((N, 8, 16, 1))], 3)
    ch = kid.reshape(N, 8, 4, P); t = tr.astype(np.float64).reshape(N, 8, 16, 4, 27)
    gi = [gentries(a).reshape(8, N - 1, G) for a in give]; ne = [gentries(a).reshape(8, 8, M) for a in near]
    y = np.zeros((N, 8, 16, 4, M), np.float64)
    for r in range(N):
        for g in range(8):
            w = [x[r, g][:, ch[r, g]]]
            for d in range(1, N):
                q = (r - d) % N
                w.append(x[q, g][:, ch[q, g][:, gi[q][g, d - 1]]])
            w = np.concatenate(w + [np.zeros((16, 4, 1))], 2)
            v = w[:, :, ne[r][g]]
            for c in range(4):
                for i, (d, s) in enumerate(FAR[c]):
                    y[r, g, :, c] += t[r, g, :, c, i, None] * v[:, s, d]
    return {"y": y.reshape(N, 128, 4 * M).astype(np.float32)}

@@ -1,0 +1,317 @@
+from concourse.mybir import AluOpType, ActivationFunctionType
+
+N = 4
+E, PAD, GH = 4096, 16, 1536
+R = E + PAD + GH
+Q = 768
+DX, DY = (-1, 0, 1, -1, 1, -1, 0, 1), (-1, -1, -1, 0, 0, 1, 1, 1)
+FAR = [[(d, s) for d in range(8) for s in range(4)
+        if max(abs(2 * DX[d] + s % 2 - c % 2), abs(2 * DY[d] + s // 2 - c // 2)) > 1] for c in range(4)]
+RELAY = (0, 1)
+
+SCRATCH = {
+    "win": ("sbuf", [128, 2 * R], "bfloat16"),
+    "kidw": ("sbuf", [128, 1544], "int32"),
+    "giv": ("sbuf", [128, 48], "int32"),
+    "nea": ("sbuf", [128, 128], "int32"),
+    "gf": ("sbuf", [128, 48], "float32"), "gq": ("sbuf", [128, 48], "int32"), "gt": ("sbuf", [128, 48], "int32"),
+    "gx": ("sbuf", [128, 48], "int32"), "gqu": ("sbuf", [128, 48], "uint16"), "gxu": ("sbuf", [128, 48], "uint16"),
+    "nf": ("sbuf", [128, 128], "float32"), "nq": ("sbuf", [128, 128], "int32"), "nt": ("sbuf", [128, 128], "int32"),
+    "nx": ("sbuf", [128, 128], "int32"), "nqu": ("sbuf", [128, 128], "uint16"), "nxu": ("sbuf", [128, 128], "uint16"),
+    "pi": ("sbuf", [128, 4], "int32"), "bi": ("sbuf", [128, 8], "int32"), "bf": ("sbuf", [128, 8], "float32"),
+    "cf": ("sbuf", [128, 8], "float32"), "cols": ("sbuf", [128, 284], "float32"),
+    "selg": ("sbuf", [128, 284], "float32"), "seln": ("sbuf", [128, 284], "float32"),
+    "rowq": ("sbuf", [128, 8], "float32"),
+    "mlo": ("sbuf", [128, 8], "bfloat16"), "mhi": ("sbuf", [128, 8], "bfloat16"), "mhf": ("sbuf", [128, 8], "float32"),
+    "ones": ("sbuf", [128, 192], "bfloat16"), "wide": ("sbuf", [128, 192], "bfloat16"),
+    "mg": ("sbuf", [128, 768], "float32"), "ag": ("sbuf", [128, 768], "float32"),
+    "mn": ("sbuf", [128, 2048], "float32"), "an": ("sbuf", [128, 2048], "float32"),
+    "og": ("sbuf", [128, 192], "uint16"), "o2": ("sbuf", [128, 512], "uint16"),
+    "gout": ("sbuf", [128, 3072], "bfloat16"),
+    "trl": ("sbuf", [128, 108], "bfloat16"), "tall": ("sbuf", [128, 128], "bfloat16"),
+    "tst": ("sbuf", [128, 128], "bfloat16"), "w8": ("sbuf", [128, 1024], "bfloat16"),
+    "wt": ("sbuf", [128, 8192], "bfloat16"),
+    "vv": ("sbuf", [128, 8192], "bfloat16"),
+    "ysb": ("sbuf", [128, 1024], "float32"),
+}
+for _k in range(8):
+    SCRATCH["ps%d" % _k] = ("psum", [128, 512], "float32")
+
+SEMAPHORES = ["cv", "ca", "ct", "cg", "dgive", "dkid", "dex0", "dex1", "dnear", "dtr", "dy", "arr", "sent", "hop"]
+
+
+def far_runs():
+    runs = []
+    for c in range(4):
+        for i, (d, s) in enumerate(FAR[c]):
+            src, dst = 27 * c + i, 32 * c + 4 * d + s
+            if runs and runs[-1][0] + runs[-1][2] == src and runs[-1][1] + runs[-1][2] == dst:
+                runs[-1][2] += 1
+            else:
+                runs.append([src, dst, 1])
+    return runs
+
+
+def helpers(T, topo, rank):
+    core, out = T.cores[rank], {}
+    for dd in RELAY:
+        dst = T.cores[(rank + dd + 1) % N]
+        out[dd] = [c for c in topo.cores_of(core) if topo.die(c) != topo.die(core) and c not in T.cores
+                   and c not in out.values() and topo.may_write(c, dst)][0]
+    return out
+
+
+def way(T, topo, rank, w, dd):
+    core = T.cores[rank]
+    if w == 0 and dd in RELAY:
+        h, dst = helpers(T, topo, rank)[dd], T.cores[(rank + dd + 1) % N]
+        return h, [e for e in topo.engines(core, h) if e not in topo.engines(core, dst)]
+    return core, []
+
+
+def hand_on(g, core, T, topo):
+    for rank in range(N):
+        for dd in RELAY:
+            h, hop = way(T, topo, rank, 0, dd)
+            if h == core:
+                dst = T.cores[(rank + dd + 1) % N]
+                rid, pid = topo.addr(dst)[0:2]
+                o = E + PAD + 512 * dd
+                g.wait_ge(T.sem.hop, len(hop))
+                g.remote_dma(T.win[:, o:o + 512], T.gout[:, 0:512], T.sem.arr, T.sem.sent, pid, rid, topo.mask(core, dst))
+                g.wait_ge(T.sem.sent, len(topo.engines(core, dst)))
+
+
+def rank_program(g, core, T, topo):
+    rank = T.rank_of(core)
+    if rank is None:
+        hand_on(g, core, T, topo)
+        return
+    A, F = AluOpType, ActivationFunctionType
+    V, S, P, Y = g.vector, g.scalar, g.tensor, g.sync
+    queue = {"cv": V, "ca": S, "ct": P, "cg": g, "sy": Y}
+    count, seen = {}, {}
+
+    def need(q, deps):
+        for sem, n in deps:
+            if seen.get((q, sem), 0) < n:
+                queue[q].wait_ge(T.sem[sem], n)
+                seen[(q, sem)] = n
+
+    def done(ins, sem, n):
+        ins.then_inc(T.sem[sem], n)
+        count[sem] = count.get(sem, 0) + n
+        return (sem, count[sem])
+
+    def ts(out, in0, s1, s2, op0, op1, *deps):
+        need("cv", deps)
+        return done(V.tensor_scalar(out, in0, s1, s2, op0) if op1 is None else V.tensor_scalar(out, in0, s1, s2, op0, op1), "cv", 1)
+
+    def tt(out, in0, in1, op, *deps):
+        need("cv", deps)
+        return done(V.tensor_tensor(out, in0, in1, op), "cv", 1)
+
+    def cp(q, out, in_, *deps):
+        need(q, deps)
+        return done(V.tensor_copy(out, in_) if q == "cv" else S.activation(out, in_, F.Copy), q, 1)
+
+    def mm(out, lhsT, rhs, start, stop, *deps):
+        need("ct", deps)
+        return done(P.matmul(out, lhsT, rhs, start, stop), "ct", 1)
+
+    def dma(q, out, in_, sem, *deps):
+        need(q, deps)
+        return done(queue[q].dma_start(out, in_), sem, 16)
+
+    def pool(ins):
+        t = done(ins, "cg", 1)
+        need("cg", [t])
+        return t
+
+    ps = [T["ps%d" % k] for k in range(8)]
+    win = T.win
+
+    d_give = dma("sy", T.giv[:], T.give[:], "dgive")
+    d_kid = dma("sy", T.kidw[:, 0:Q], T.kid[:], "dkid")
+    d_ex = [dma("sy", win[:, 0:E], T.ex[:], "dex0")]
+    dma("sy", win[0:64, R:R + E], T.ex[64:128, :], "dex1")
+    d_ex.append(dma("sy", win[64:128, R:R + E], T.ex[0:64, :], "dex1"))
+    d_tr = dma("ca", T.trl[:], T.tr[:], "dtr")
+    d_near = dma("ca", T.nea[:], T.near[:], "dnear")
+
+    g_pi = pool(g.iota(T.pi[:, 0:1], [[0, 1]], 0, 1))
+    g_cols = pool(g.iota(T.cols[:], [[1, 284]], -14, 0, allow_small_or_imprecise_dtypes=True))
+    g_gh = pool(g.iota(T.kidw[:, Q:2 * Q], [[2, Q]], E + PAD, 0))
+    pool(g.iota(T.ones[:], [[0, 192]], 1, 0, allow_small_or_imprecise_dtypes=True))
+    for b in range(2):
+        g_wide = pool(g.affine_select(T.wide[64 * b:64 * b + 64, :], T.ones[64 * b:64 * b + 64, :], [[-1, 192]],
+                                      A.is_equal, 0.0, 64, 1))
+
+    v_tz = done(V.memset(T.tall[:], 0.0), "cv", 1)
+    done(V.memset(win[:, E:E + PAD], 0.0), "cv", 1)
+    done(V.memset(win[:, R + E:R + E + PAD], 0.0), "cv", 1)
+    v_zero = done(V.memset(T.kidw[:, 2 * Q:2 * Q + 8], E), "cv", 1)
+    pi, bi, bf, cf = T.pi[:, 0:1], T.bi, T.bf, T.cf
+    for k, (sh, mask) in enumerate([(0, 48), (3, 1), (2, 1), (6, 1), (0, 3), (0, 7), (3, 7)]):
+        t = ts(bi[:, k:k + 1], pi, sh, mask, A.logical_shift_right, A.bitwise_and, g_pi)
+    v_bf = cp("cv", bf[:, 0:7], bi[:, 0:7], t)
+    k16, cb_, sp_, a_, q_, xlo, xhi = [bf[:, k:k + 1] for k in range(7)]
+    v_rowq = ts(T.rowq[:], T.cols[:, 14:22], 3.0, q_, A.min, A.is_equal, v_bf, g_cols)
+    ts(cf[:, 0:1], cb_, 64.0, k16, A.mult, A.add)
+    t = ts(cf[:, 1:2], a_, cb_, 142.0, A.not_equal, A.mult)
+    ts(cf[:, 3:4], a_, 142.0, cf[:, 0:1], A.mult, A.add, t)
+    v_cf = ts(cf[:, 2:3], cf[:, 0:1], cf[:, 1:2], None, A.add, None)
+    v_selg = ts(T.selg[:], T.cols[:], sp_, cf[:, 2:3], A.subtract, A.is_equal, v_cf)
+    v_seln = ts(T.seln[:], T.cols[:], sp_, cf[:, 3:4], A.subtract, A.is_equal)
+
+    def quarter(n, f, qi, qu, loaded):
+        t0 = ts(f[:], n[:], -383.6, 1.0 / Q, A.add, A.mult, loaded)
+        t1 = cp("cv", qi[:], f[:], t0)
+        return cp("cv", qu[:], qi[:], t1)
+
+    def place(n, qi, t_, x, xu):
+        t2 = ts(t_[:], qi[:], 3.0, -float(Q), A.min, A.mult)
+        t3 = tt(x[:], n[:], t_[:], A.add, t2)
+        return cp("cv", xu[:], x[:], t3)
+
+    v_gq = quarter(T.giv, T.gf, T.gq, T.gqu, d_give)
+    v_gx = place(T.giv, T.gq, T.gt, T.gx, T.gxu)
+    v_nq = quarter(T.nea, T.nf, T.nq, T.nqu, d_near)
+
+    runs = far_runs()
+
+    def spread(part):
+        return [cp("ca", T.tall[:, dst:dst + n], T.trl[:, src:src + n], d_tr, v_tz) for src, dst, n in part][-1]
+
+    spread(runs[:7])
+
+    a_mg = [cp("ca", T.mg[:, 384 * k:384 * k + 384], T.rowq[:].indirect(T.gqu[:, 24 * k:24 * k + 24]), v_rowq, v_gq)
+            for k in range(2)]
+    for k in range(2):
+        v_ag = tt(T.ag[:, 384 * k:384 * k + 384], T.kidw[:, 0:Q].indirect(T.gxu[:, 24 * k:24 * k + 24]),
+                  T.mg[:, 384 * k:384 * k + 384], A.mult, d_kid, v_gx, a_mg[k])
+    t_og = []
+    for w in range(2):
+        for jj in range(8):
+            o = 142 * w + 14 - 2 * jj
+            t = mm(ps[4 + w][:, 0:96], T.selg[:, o:o + 128], T.ag[:, jj::8], jj == 0, jj == 7, v_selg, v_ag)
+        t_og.append(t)
+
+    def mask_near(k):
+        return cp("ca", T.mn[:, 512 * k:512 * k + 512], T.rowq[:].indirect(T.nqu[:, 32 * k:32 * k + 32]), v_nq)
+
+    def list_near(k, m):
+        va = tt(T.an[:, 512 * k:512 * k + 512], T.kidw[:, 0:1544].indirect(T.nxu[:, 32 * k:32 * k + 32]),
+                T.mn[:, 512 * k:512 * k + 512], A.mult, v_nx, v_ghost, m)
+        for a in range(2):
+            o = 128 * a + 64 * (k % 2)
+            for jj in range(8):
+                c = 142 * a + 14 - 2 * jj
+                t = mm(ps[6 + k // 2][:, o:o + 64], T.seln[:, c:c + 128], T.an[:, 512 * k + jj:512 * k + 512:8],
+                       jj == 0, jj == 7, v_seln, va)
+        return t
+
+    def deal_near(h, formed):
+        for a in range(2):
+            t = ts(T.o2[:, 256 * a + 128 * h:256 * a + 128 * h + 128], ps[6 + h][:, 128 * a:128 * a + 128],
+                   cf[:, 4 + a:5 + a], None, A.add, None, formed)
+        return t
+
+    def gather_give(q, w, c0, c1, listed):
+        return cp(q, T.gout[:, 1536 * w + 16 * c0:1536 * w + 16 * c1],
+                  win[:, R * w:R * w + E + PAD].indirect(T.og[:, 96 * w + c0:96 * w + c1]), listed, d_ex[w], v_zero)
+
+    def send(w, dd, deps):
+        need("cg", deps)
+        piece = T.gout[:, 1536 * w + 512 * dd:1536 * w + 512 * dd + 512]
+        h, hop = way(T, topo, rank, w, dd)
+        if hop:
+            rid, pid = topo.addr(h)[0:2]
+            g.remote_dma(T.gout[:, 0:512], piece, T.sem.hop, T.sem.sent, pid, rid, sum(1 << e for e in hop))
+        else:
+            dst = T.cores[(rank + dd + 1) % N]
+            assert topo.may_write(core, dst)
+            rid, pid = topo.addr(dst)[0:2]
+            o = R * w + E + PAD + 512 * dd
+            hop = topo.engines(core, dst)
+            g.remote_dma(win[:, o:o + 512], piece, T.sem.arr, T.sem.sent, pid, rid, topo.mask(core, dst))
+        count["sent"] = count.get("sent", 0) + len(hop)
+        writer = way(T, topo, (rank - dd - 1) % N, w, dd)[0]
+        count["arr"] = count.get("arr", 0) + len(topo.engines(writer, core))
+
+    a_mn = [mask_near(0), mask_near(1)]
+    a_tall = spread(runs[7:])
+    t_tst = a_tall
+    for a in range(2):
+        before = t_tst
+        for cb in range(2):
+            for sp in range(2):
+                for b in range(2):
+                    o = 64 * cb + 32 * a + 16 * sp
+                    t_tst = mm(ps[0][:, o:o + 16], T.wide[64 * a:64 * a + 64, 64 - 64 * b:192 - 64 * b],
+                               T.tall[64 * a:64 * a + 64, 64 * cb + 2 * b + sp:64 * cb + 64:4], b == 0, b == 1, g_wide, before)
+    v_nx = place(T.nea, T.nq, T.nt, T.nx, T.nxu)
+    v_ghost = ts(T.kidw[:, Q:2 * Q], T.kidw[:, Q:2 * Q], sp_, None, A.add, None, g_gh)
+    ts(cf[:, 4:5], a_, float(R), None, A.mult, None)
+    ts(cf[:, 5:6], a_, -float(R), float(R), A.mult, A.add)
+    v_og0 = cp("cv", T.og[:, 0:96], ps[4][:, 0:96], t_og[0])
+    for dd in range(N - 1):
+        send(0, dd, [gather_give("cv", 0, 32 * dd, 32 * dd + 16, v_og0), gather_give("ca", 0, 32 * dd + 16, 32 * dd + 32, v_og0)])
+    v_og1 = cp("cv", T.og[:, 96:192], ps[5][:, 0:96], t_og[1])
+    a_mn.append(mask_near(2))
+    list_near(0, a_mn[0])
+    t_n1 = list_near(1, a_mn[1])
+    send(1, 0, [gather_give("ca", 1, 0, 32, v_og1)])
+    send(1, 1, [gather_give("cv", 1, 32, 64, v_og1)])
+    send(1, 2, [gather_give("ca", 1, 64, 96, v_og1)])
+    a_mn.append(mask_near(3))
+
+    ts(T.mlo[:], T.cols[:, 14:22], xlo, None, A.is_equal, None)
+    ts(T.mhi[:], T.cols[:, 14:22], xhi, None, A.is_equal, None)
+    ts(T.mhf[:], T.cols[:, 14:22], xhi, None, A.is_equal, None)
+    v_tst = cp("cv", T.tst[:], ps[0][:, 0:128], t_tst)
+    for k in range(8):
+        v_w8 = ts(T.w8[:, 128 * k:128 * k + 128], T.tst[:], T.mlo[:, k:k + 1], None, A.mult, None, v_tst)
+    list_near(2, a_mn[2])
+    t_n3 = list_near(3, a_mn[3])
+    v_o = [deal_near(0, t_n1)]
+    for k in range(8):
+        out = T.wt[:, 1024 * k:1024 * k + 1024]
+        if k < 4:
+            need("ca", [v_w8])
+            a_wt = done(S.activation(out, T.w8[:], F.Copy, scale=T.mhf[:, k:k + 1]), "ca", 1)
+        else:
+            v_wt = ts(out, T.w8[:], T.mhi[:, k:k + 1], None, A.mult, None, v_w8)
+    v_o.append(deal_near(1, t_n3))
+
+    arrived = ("arr", count["arr"])
+    last = {}
+
+    def colleagues(a, d):
+        o, l0 = 4096 * a + 512 * d, 256 * a + 32 * d
+        if (a, d) in ((0, 0), (1, 7)):
+            got = [cp(q, T.vv[:, o + 256 * k:o + 256 * k + 256], win[:].indirect(T.o2[:, l0 + 16 * k:l0 + 16 * k + 16]),
+                      arrived, v_o[d // 4], d_ex[0], d_ex[1]) for k, q in enumerate(("cv", "ca"))]
+        else:
+            got = [cp("cv" if d % 2 else "ca", T.vv[:, o:o + 512], win[:].indirect(T.o2[:, l0:l0 + 32]), v_o[d // 4])]
+        for sp in range(2):
+            for ch in range(2):
+                if any((d, sp + 2 * b) in FAR[ch + 2 * cb] for b in range(2) for cb in range(2)):
+                    m = 32 * a + 16 * sp + 8 * ch + d
+                    last[(a, ch)] = mm(ps[2 * a + ch][:, 0:256], T.wt[:, m::64], T.vv[:, o + sp:o + 512:2],
+                                       (d, sp) == (0, 0), (d, sp) == (7, 1), a_wt, v_wt, *got)
+
+    def store(a):
+        out = [cp("cv" if ch else "ca", T.ysb[:, 512 * a + 256 * ch:512 * a + 256 * ch + 256], ps[2 * a + ch][:, 0:256],
+                  last[(a, ch)]) for ch in range(2)]
+        dma("sy", T.y[64 * a:64 * a + 64, :], T.ysb[:, 512 * a:512 * a + 512], "dy", *out)
+
+    for d in range(8):
+        colleagues(0, d)
+    for d in range(8):
+        if d == 4:
+            store(0)
+        colleagues(1, d)
+    store(1)
+
+    need("cg", sorted(count.items()))

@@ -7,20 +7,22 @@ Q = 768
 DX, DY = (-1, 0, 1, -1, 1, -1, 0, 1), (-1, -1, -1, 0, 0, 1, 1, 1)
 FAR = [[(d, s) for d in range(8) for s in range(4)
         if max(abs(2 * DX[d] + s % 2 - c % 2), abs(2 * DY[d] + s // 2 - c // 2)) > 1] for c in range(4)]
-RELAY = (0, 1)
+RELAY = ((1, 0), (1, 1))
+W0 = 3
+VD = ((0, 5), (0, 7), (1, 1), (1, 3), (1, 5))
 
 SCRATCH = {
     "win": ("sbuf", [128, 2 * R], "bfloat16"),
     "kidw": ("sbuf", [128, 1544], "int32"),
     "giv": ("sbuf", [128, 48], "int32"),
     "nea": ("sbuf", [128, 128], "int32"),
-    "gf": ("sbuf", [128, 48], "float32"), "gq": ("sbuf", [128, 48], "int32"), "gt": ("sbuf", [128, 48], "int32"),
-    "gx": ("sbuf", [128, 48], "int32"), "gqu": ("sbuf", [128, 48], "uint16"), "gxu": ("sbuf", [128, 48], "uint16"),
-    "nf": ("sbuf", [128, 128], "float32"), "nq": ("sbuf", [128, 128], "int32"), "nt": ("sbuf", [128, 128], "int32"),
-    "nx": ("sbuf", [128, 128], "int32"), "nqu": ("sbuf", [128, 128], "uint16"), "nxu": ("sbuf", [128, 128], "uint16"),
+    "gt": ("sbuf", [128, 48], "int32"), "gx": ("sbuf", [128, 48], "int32"),
+    "gqu": ("sbuf", [128, 48], "uint16"), "gxu": ("sbuf", [128, 48], "uint16"),
+    "nt": ("sbuf", [128, 128], "int32"), "nx": ("sbuf", [128, 128], "int32"),
+    "nqu": ("sbuf", [128, 128], "uint16"), "nxu": ("sbuf", [128, 128], "uint16"),
     "pi": ("sbuf", [128, 4], "int32"), "bi": ("sbuf", [128, 8], "int32"), "bf": ("sbuf", [128, 8], "float32"),
     "cf": ("sbuf", [128, 8], "float32"), "cols": ("sbuf", [128, 284], "float32"),
-    "selg": ("sbuf", [128, 284], "float32"), "seln": ("sbuf", [128, 284], "float32"),
+    "sel": ("sbuf", [128, 284], "float32"),
     "rowq": ("sbuf", [128, 8], "float32"),
     "mlo": ("sbuf", [128, 8], "bfloat16"), "mhi": ("sbuf", [128, 8], "bfloat16"), "mhf": ("sbuf", [128, 8], "float32"),
     "ones": ("sbuf", [128, 192], "bfloat16"), "wide": ("sbuf", [128, 192], "bfloat16"),
@@ -37,7 +39,8 @@ SCRATCH = {
 for _k in range(8):
     SCRATCH["ps%d" % _k] = ("psum", [128, 512], "float32")
 
-SEMAPHORES = ["cv", "ca", "ct", "cg", "dgive", "dkid", "dex0", "dex1", "dnear", "dtr", "dy", "arr", "sent", "hop"]
+SEMAPHORES = ["cv", "ca", "ct", "cg", "dgive", "dkid", "dex0", "dex1", "dnear", "dtr", "dy",
+              "arr0", "arr1", "sent", "hop0", "hop1"]
 
 
 def far_runs():
@@ -52,34 +55,33 @@ def far_runs():
     return runs
 
 
-def helpers(T, topo, rank):
+def way(T, topo, rank, a, dd):
     core, out = T.cores[rank], {}
-    for dd in RELAY:
-        dst = T.cores[(rank + dd + 1) % N]
-        out[dd] = [c for c in topo.cores_of(core) if topo.die(c) != topo.die(core) and c not in T.cores
-                   and c not in out.values() and topo.may_write(c, dst)][0]
-    return out
-
-
-def way(T, topo, rank, w, dd):
-    core = T.cores[rank]
-    if w == 0 and dd in RELAY:
-        h, dst = helpers(T, topo, rank)[dd], T.cores[(rank + dd + 1) % N]
-        return h, [e for e in topo.engines(core, h) if e not in topo.engines(core, dst)]
-    return core, []
+    if (a, dd) not in RELAY:
+        return core, []
+    for k in sorted(set(x[1] for x in RELAY)):
+        dst = T.cores[(rank + k + 1) % N]
+        out[k] = [c for c in topo.cores_of(core) if topo.die(c) != topo.die(core) and c not in T.cores
+                  and c not in out.values() and topo.may_write(c, dst)][0]
+    dst = T.cores[(rank + dd + 1) % N]
+    return out[dd], [e for e in topo.engines(core, out[dd]) if e not in topo.engines(core, dst)]
 
 
 def hand_on(g, core, T, topo):
+    sent = 0
     for rank in range(N):
-        for dd in RELAY:
-            h, hop = way(T, topo, rank, 0, dd)
+        for a, dd in RELAY:
+            h, hop = way(T, topo, rank, a, dd)
             if h == core:
                 dst = T.cores[(rank + dd + 1) % N]
                 rid, pid = topo.addr(dst)[0:2]
-                o = E + PAD + 512 * dd
-                g.wait_ge(T.sem.hop, len(hop))
-                g.remote_dma(T.win[:, o:o + 512], T.gout[:, 0:512], T.sem.arr, T.sem.sent, pid, rid, topo.mask(core, dst))
-                g.wait_ge(T.sem.sent, len(topo.engines(core, dst)))
+                o = R * a + E + PAD + 512 * dd
+                g.wait_ge(T.sem["hop%d" % a], len(hop))
+                g.remote_dma(T.win[:, o:o + 512], T.gout[:, 512 * a:512 * a + 512], T.sem["arr%d" % a], T.sem.sent,
+                             pid, rid, topo.mask(core, dst))
+                sent += len(topo.engines(core, dst))
+    if sent:
+        g.wait_ge(T.sem.sent, sent)
 
 
 def rank_program(g, core, T, topo):
@@ -133,183 +135,199 @@ def rank_program(g, core, T, topo):
 
     d_give = dma("sy", T.giv[:], T.give[:], "dgive")
     d_kid = dma("sy", T.kidw[:, 0:Q], T.kid[:], "dkid")
-    d_ex = [dma("sy", win[:, 0:E], T.ex[:], "dex0")]
-    dma("sy", win[0:64, R:R + E], T.ex[64:128, :], "dex1")
-    d_ex.append(dma("sy", win[64:128, R:R + E], T.ex[0:64, :], "dex1"))
+    d_ex = [[dma("sy", win[64 * b:64 * b + 64, R * a:R * a + E], T.ex[64 * a:64 * a + 64, :], "dex%d" % a)
+             for b in range(2)][1] for a in range(2)]
     d_tr = dma("ca", T.trl[:], T.tr[:], "dtr")
     d_near = dma("ca", T.nea[:], T.near[:], "dnear")
 
     g_pi = pool(g.iota(T.pi[:, 0:1], [[0, 1]], 0, 1))
     g_cols = pool(g.iota(T.cols[:], [[1, 284]], -14, 0, allow_small_or_imprecise_dtypes=True))
-    g_gh = pool(g.iota(T.kidw[:, Q:2 * Q], [[2, Q]], E + PAD, 0))
+    pool(g.iota(win[:, E:E + PAD], [[0, PAD]], 0, 0, allow_small_or_imprecise_dtypes=True))
+    pool(g.iota(win[:, R + E:R + E + PAD], [[0, PAD]], 0, 0, allow_small_or_imprecise_dtypes=True))
+    g_zero = pool(g.iota(T.kidw[:, 2 * Q:2 * Q + 8], [[0, 8]], E, 0))
     pool(g.iota(T.ones[:], [[0, 192]], 1, 0, allow_small_or_imprecise_dtypes=True))
     for b in range(2):
         g_wide = pool(g.affine_select(T.wide[64 * b:64 * b + 64, :], T.ones[64 * b:64 * b + 64, :], [[-1, 192]],
                                       A.is_equal, 0.0, 64, 1))
 
     v_tz = done(V.memset(T.tall[:], 0.0), "cv", 1)
-    done(V.memset(win[:, E:E + PAD], 0.0), "cv", 1)
-    done(V.memset(win[:, R + E:R + E + PAD], 0.0), "cv", 1)
-    v_zero = done(V.memset(T.kidw[:, 2 * Q:2 * Q + 8], E), "cv", 1)
     pi, bi, bf, cf = T.pi[:, 0:1], T.bi, T.bf, T.cf
     for k, (sh, mask) in enumerate([(0, 48), (3, 1), (2, 1), (6, 1), (0, 3), (0, 7), (3, 7)]):
         t = ts(bi[:, k:k + 1], pi, sh, mask, A.logical_shift_right, A.bitwise_and, g_pi)
     v_bf = cp("cv", bf[:, 0:7], bi[:, 0:7], t)
     k16, cb_, sp_, a_, q_, xlo, xhi = [bf[:, k:k + 1] for k in range(7)]
-    v_rowq = ts(T.rowq[:], T.cols[:, 14:22], 3.0, q_, A.min, A.is_equal, v_bf, g_cols)
-    ts(cf[:, 0:1], cb_, 64.0, k16, A.mult, A.add)
-    t = ts(cf[:, 1:2], a_, cb_, 142.0, A.not_equal, A.mult)
-    ts(cf[:, 3:4], a_, 142.0, cf[:, 0:1], A.mult, A.add, t)
-    v_cf = ts(cf[:, 2:3], cf[:, 0:1], cf[:, 1:2], None, A.add, None)
-    v_selg = ts(T.selg[:], T.cols[:], sp_, cf[:, 2:3], A.subtract, A.is_equal, v_cf)
-    v_seln = ts(T.seln[:], T.cols[:], sp_, cf[:, 3:4], A.subtract, A.is_equal)
+    t = ts(cf[:, 0:1], cb_, 64.0, k16, A.mult, A.add, v_bf)
+    for k in range(3):
+        ts(cf[:, 2 + k:3 + k], sp_, float(E + PAD + 512 * k), None, A.add, None)
+    v_cf = ts(cf[:, 1:2], a_, 142.0, cf[:, 0:1], A.mult, A.add, t)
+    v_rowq = ts(T.rowq[:], T.cols[:, 14:22], 3.0, q_, A.min, A.is_equal, g_cols)
+    v_sel = ts(T.sel[:], T.cols[:], sp_, cf[:, 1:2], A.subtract, A.is_equal, v_cf)
 
-    def quarter(n, f, qi, qu, loaded):
-        t0 = ts(f[:], n[:], -383.6, 1.0 / Q, A.add, A.mult, loaded)
-        t1 = cp("cv", qi[:], f[:], t0)
-        return cp("cv", qu[:], qi[:], t1)
+    def ghosts(k):
+        return ts(T.kidw[:, Q + 256 * k:Q + 256 * k + 256], T.cols[:, 14:270], 2.0, cf[:, 2 + k:3 + k], A.mult, A.add)
 
-    def place(n, qi, t_, x, xu):
-        t2 = ts(t_[:], qi[:], 3.0, -float(Q), A.min, A.mult)
+    def quarter(n, qu, loaded):
+        return ts(qu[:], n[:], -383.6, 1.0 / Q, A.add, A.mult, loaded)
+
+    def place(n, qu, t_, x, xu, have):
+        t2 = ts(t_[:], qu[:], 3.0, -float(Q), A.min, A.mult, have)
         t3 = tt(x[:], n[:], t_[:], A.add, t2)
         return cp("cv", xu[:], x[:], t3)
 
-    v_gq = quarter(T.giv, T.gf, T.gq, T.gqu, d_give)
-    v_gx = place(T.giv, T.gq, T.gt, T.gx, T.gxu)
-    v_nq = quarter(T.nea, T.nf, T.nq, T.nqu, d_near)
+    ghosts(0)
+    ghosts(1)
+    v_gq = quarter(T.giv, T.gqu, d_give)
+    v_ghost = ghosts(2)
+    v_gx = place(T.giv, T.gqu, T.gt, T.gx, T.gxu, v_gq)
+    v_nq = quarter(T.nea, T.nqu, d_near)
 
     runs = far_runs()
 
     def spread(part):
         return [cp("ca", T.tall[:, dst:dst + n], T.trl[:, src:src + n], d_tr, v_tz) for src, dst, n in part][-1]
 
-    spread(runs[:7])
+    spread(runs[:5])
 
     a_mg = [cp("ca", T.mg[:, 384 * k:384 * k + 384], T.rowq[:].indirect(T.gqu[:, 24 * k:24 * k + 24]), v_rowq, v_gq)
             for k in range(2)]
-    for k in range(2):
-        v_ag = tt(T.ag[:, 384 * k:384 * k + 384], T.kidw[:, 0:Q].indirect(T.gxu[:, 24 * k:24 * k + 24]),
-                  T.mg[:, 384 * k:384 * k + 384], A.mult, d_kid, v_gx, a_mg[k])
+    v_nx = place(T.nea, T.nqu, T.nt, T.nx, T.nxu, v_nq)
+    v_ag = [tt(T.ag[:, 384 * k:384 * k + 384], T.kidw[:, 0:Q].indirect(T.gxu[:, 24 * k:24 * k + 24]),
+               T.mg[:, 384 * k:384 * k + 384], A.mult, d_kid, v_gx, a_mg[k]) for k in range(2)]
     t_og = []
-    for w in range(2):
-        for jj in range(8):
-            o = 142 * w + 14 - 2 * jj
-            t = mm(ps[4 + w][:, 0:96], T.selg[:, o:o + 128], T.ag[:, jj::8], jj == 0, jj == 7, v_selg, v_ag)
+    for a in range(2):
+        for k0, k1 in ((0, 1), (1, 2)) if a == 0 else ((0, 2),):
+            for jj in range(8):
+                o = 142 * a + 14 - 2 * jj
+                t = mm(ps[4 + a][:, 48 * k0:48 * k1], T.sel[:, o:o + 128], T.ag[:, 384 * k0 + jj:384 * k1:8],
+                       jj == 0, jj == 7, v_sel, v_ag[k1 - 1])
         t_og.append(t)
 
     def mask_near(k):
         return cp("ca", T.mn[:, 512 * k:512 * k + 512], T.rowq[:].indirect(T.nqu[:, 32 * k:32 * k + 32]), v_nq)
 
-    def list_near(k, m):
-        va = tt(T.an[:, 512 * k:512 * k + 512], T.kidw[:, 0:1544].indirect(T.nxu[:, 32 * k:32 * k + 32]),
-                T.mn[:, 512 * k:512 * k + 512], A.mult, v_nx, v_ghost, m)
-        for a in range(2):
-            o = 128 * a + 64 * (k % 2)
-            for jj in range(8):
-                c = 142 * a + 14 - 2 * jj
-                t = mm(ps[6 + k // 2][:, o:o + 64], T.seln[:, c:c + 128], T.an[:, 512 * k + jj:512 * k + 512:8],
-                       jj == 0, jj == 7, v_seln, va)
+    def kids_near(k, m):
+        return tt(T.an[:, 512 * k:512 * k + 512], T.kidw[:, 0:1544].indirect(T.nxu[:, 32 * k:32 * k + 32]),
+                  T.mn[:, 512 * k:512 * k + 512], A.mult, v_nx, v_ghost, g_zero, m)
+
+    def bank(a, h):
+        return ps[6 + a - 2 * h]
+
+    def list_near(a, k, *deps):
+        for jj in range(8):
+            c = 142 * a + 14 - 2 * jj
+            t = mm(bank(a, k // 2)[:, 64 * (k % 2):64 * (k % 2) + 64], T.sel[:, c:c + 128],
+                   T.an[:, 512 * k + jj:512 * k + 512:8], jj == 0, jj == 7, *deps)
         return t
 
-    def deal_near(h, formed):
-        for a in range(2):
-            t = ts(T.o2[:, 256 * a + 128 * h:256 * a + 128 * h + 128], ps[6 + h][:, 128 * a:128 * a + 128],
-                   cf[:, 4 + a:5 + a], None, A.add, None, formed)
-        return t
+    def deal_near(a, h, formed):
+        return cp("cv", T.o2[:, 256 * a + 128 * h:256 * a + 128 * h + 128], bank(a, h)[:, 0:128], formed)
 
-    def gather_give(q, w, c0, c1, listed):
-        return cp(q, T.gout[:, 1536 * w + 16 * c0:1536 * w + 16 * c1],
-                  win[:, R * w:R * w + E + PAD].indirect(T.og[:, 96 * w + c0:96 * w + c1]), listed, d_ex[w], v_zero)
+    def gather_give(q, a, c0, c1, listed):
+        return cp(q, T.gout[:, 1536 * a + 16 * c0:1536 * a + 16 * c1],
+                  win[:, R * a:R * a + E + PAD].indirect(T.og[:, 96 * a + c0:96 * a + c1]), listed, d_ex[a], g_zero)
 
-    def send(w, dd, deps):
+    def send(a, dd, deps):
         need("cg", deps)
-        piece = T.gout[:, 1536 * w + 512 * dd:1536 * w + 512 * dd + 512]
-        h, hop = way(T, topo, rank, w, dd)
+        piece = T.gout[:, 1536 * a + 512 * dd:1536 * a + 512 * dd + 512]
+        h, hop = way(T, topo, rank, a, dd)
         if hop:
             rid, pid = topo.addr(h)[0:2]
-            g.remote_dma(T.gout[:, 0:512], piece, T.sem.hop, T.sem.sent, pid, rid, sum(1 << e for e in hop))
+            g.remote_dma(T.gout[:, 512 * a:512 * a + 512], piece, T.sem["hop%d" % a], T.sem.sent, pid, rid,
+                         sum(1 << e for e in hop))
         else:
             dst = T.cores[(rank + dd + 1) % N]
             assert topo.may_write(core, dst)
             rid, pid = topo.addr(dst)[0:2]
-            o = R * w + E + PAD + 512 * dd
+            o = R * a + E + PAD + 512 * dd
             hop = topo.engines(core, dst)
-            g.remote_dma(win[:, o:o + 512], piece, T.sem.arr, T.sem.sent, pid, rid, topo.mask(core, dst))
+            g.remote_dma(win[:, o:o + 512], piece, T.sem["arr%d" % a], T.sem.sent, pid, rid, topo.mask(core, dst))
         count["sent"] = count.get("sent", 0) + len(hop)
-        writer = way(T, topo, (rank - dd - 1) % N, w, dd)[0]
-        count["arr"] = count.get("arr", 0) + len(topo.engines(writer, core))
+        writer = way(T, topo, (rank - dd - 1) % N, a, dd)[0]
+        count["arr%d" % a] = count.get("arr%d" % a, 0) + len(topo.engines(writer, core))
 
     a_mn = [mask_near(0), mask_near(1)]
-    a_tall = spread(runs[7:])
-    t_tst = a_tall
+    a_tall = spread(runs[5:])
+    t_tst = []
     for a in range(2):
-        before = t_tst
         for cb in range(2):
             for sp in range(2):
                 for b in range(2):
-                    o = 64 * cb + 32 * a + 16 * sp
-                    t_tst = mm(ps[0][:, o:o + 16], T.wide[64 * a:64 * a + 64, 64 - 64 * b:192 - 64 * b],
-                               T.tall[64 * a:64 * a + 64, 64 * cb + 2 * b + sp:64 * cb + 64:4], b == 0, b == 1, g_wide, before)
-    v_nx = place(T.nea, T.nq, T.nt, T.nx, T.nxu)
-    v_ghost = ts(T.kidw[:, Q:2 * Q], T.kidw[:, Q:2 * Q], sp_, None, A.add, None, g_gh)
-    ts(cf[:, 4:5], a_, float(R), None, A.mult, None)
-    ts(cf[:, 5:6], a_, -float(R), float(R), A.mult, A.add)
-    v_og0 = cp("cv", T.og[:, 0:96], ps[4][:, 0:96], t_og[0])
-    for dd in range(N - 1):
-        send(0, dd, [gather_give("cv", 0, 32 * dd, 32 * dd + 16, v_og0), gather_give("ca", 0, 32 * dd + 16, 32 * dd + 32, v_og0)])
-    v_og1 = cp("cv", T.og[:, 96:192], ps[5][:, 0:96], t_og[1])
-    a_mn.append(mask_near(2))
-    list_near(0, a_mn[0])
-    t_n1 = list_near(1, a_mn[1])
-    send(1, 0, [gather_give("ca", 1, 0, 32, v_og1)])
-    send(1, 1, [gather_give("cv", 1, 32, 64, v_og1)])
-    send(1, 2, [gather_give("ca", 1, 64, 96, v_og1)])
-    a_mn.append(mask_near(3))
+                    o = 32 * cb + 16 * sp
+                    t = mm(ps[2 * a][:, o:o + 16], T.wide[64 * a:64 * a + 64, 64 - 64 * b:192 - 64 * b],
+                           T.tall[64 * a:64 * a + 64, 64 * cb + 2 * b + sp:64 * cb + 64:4], b == 0, b == 1, g_wide, a_tall)
+        t_tst.append(t)
+
+    def weights8(a):
+        t = cp("cv", T.tst[:, 64 * a:64 * a + 64], ps[2 * a][:, 0:64], t_tst[a])
+        return [ts(T.w8[:, 512 * a + 64 * k:512 * a + 64 * k + 64], T.tst[:, 64 * a:64 * a + 64], T.mlo[:, k:k + 1], None,
+                   A.mult, None, t) for k in range(8)][-1]
+
+    def weights(a, q, ks, w8):
+        need(q, [w8])
+        for k in ks:
+            out, src = T.wt[:, 4096 * a + 512 * k:4096 * a + 512 * k + 512], T.w8[:, 512 * a:512 * a + 512]
+            if q == "ca":
+                t = done(S.activation(out, src, F.Copy, scale=T.mhf[:, k:k + 1]), "ca", 1)
+            else:
+                t = ts(out, src, T.mhi[:, k:k + 1], None, A.mult, None)
+        return t
 
     ts(T.mlo[:], T.cols[:, 14:22], xlo, None, A.is_equal, None)
     ts(T.mhi[:], T.cols[:, 14:22], xhi, None, A.is_equal, None)
     ts(T.mhf[:], T.cols[:, 14:22], xhi, None, A.is_equal, None)
-    v_tst = cp("cv", T.tst[:], ps[0][:, 0:128], t_tst)
-    for k in range(8):
-        v_w8 = ts(T.w8[:, 128 * k:128 * k + 128], T.tst[:], T.mlo[:, k:k + 1], None, A.mult, None, v_tst)
-    list_near(2, a_mn[2])
-    t_n3 = list_near(3, a_mn[3])
-    v_o = [deal_near(0, t_n1)]
-    for k in range(8):
-        out = T.wt[:, 1024 * k:1024 * k + 1024]
-        if k < 4:
-            need("ca", [v_w8])
-            a_wt = done(S.activation(out, T.w8[:], F.Copy, scale=T.mhf[:, k:k + 1]), "ca", 1)
-        else:
-            v_wt = ts(out, T.w8[:], T.mhi[:, k:k + 1], None, A.mult, None, v_w8)
-    v_o.append(deal_near(1, t_n3))
+    t_n, v_an = {}, [kids_near(0, a_mn[0])]
+    v_og0 = cp("cv", T.og[:, 0:96], ps[4][:, 0:96], t_og[0])
+    for dd in range(N - 1):
+        send(0, dd, [gather_give("cv", 0, 32 * dd, 32 * dd + 16, v_og0), gather_give("ca", 0, 32 * dd + 16, 32 * dd + 32, v_og0)])
+    v_og1 = cp("cv", T.og[:, 96:192], ps[5][:, 0:96], t_og[1])
+    a_mn += [mask_near(2), mask_near(3)]
+    v_an += [kids_near(1, a_mn[1]), kids_near(2, a_mn[2])]
+    for k in range(2):
+        t_n[0, k] = list_near(0, k, v_an[k])
+        t_n[1, k] = list_near(1, k)
+    send(1, 0, [gather_give("ca", 1, 0, 32, v_og1)])
+    send(1, 1, [gather_give("cv", 1, 32, 64, v_og1)])
+    send(1, 2, [gather_give("ca", 1, 64, 96, v_og1)])
+    v_w8 = [weights8(0)]
+    v_an.append(kids_near(3, a_mn[3]))
+    for k in range(2, 4):
+        t_n[0, k] = list_near(0, k, v_an[k], v_og0)
+    for k in range(2, 4):
+        t_n[1, k] = list_near(1, k, v_og1)
+    v_o = {(0, 0): deal_near(0, 0, t_n[0, 1])}
+    made = [[weights(0, "ca", range(W0), v_w8[0]), weights(0, "cv", range(W0, 8), v_w8[0])]]
+    v_o[0, 1] = deal_near(0, 1, t_n[0, 3])
 
-    arrived = ("arr", count["arr"])
     last = {}
 
     def colleagues(a, d):
-        o, l0 = 4096 * a + 512 * d, 256 * a + 32 * d
-        if (a, d) in ((0, 0), (1, 7)):
-            got = [cp(q, T.vv[:, o + 256 * k:o + 256 * k + 256], win[:].indirect(T.o2[:, l0 + 16 * k:l0 + 16 * k + 16]),
-                      arrived, v_o[d // 4], d_ex[0], d_ex[1]) for k, q in enumerate(("cv", "ca"))]
+        o, l0, w = 4096 * a + 512 * d, 256 * a + 32 * d, win[:, R * a:R * a + R]
+        deps = [("arr%d" % a, count["arr%d" % a]), v_o[a, d // 4], d_ex[a]]
+        if (a, d) == (1, 7):
+            got = [cp(q, T.vv[:, o + 256 * k:o + 256 * k + 256], w.indirect(T.o2[:, l0 + 16 * k:l0 + 16 * k + 16]), *deps)
+                   for k, q in enumerate(("cv", "ca"))]
         else:
-            got = [cp("cv" if d % 2 else "ca", T.vv[:, o:o + 512], win[:].indirect(T.o2[:, l0:l0 + 32]), v_o[d // 4])]
+            got = [cp("cv" if (a, d) in VD else "ca", T.vv[:, o:o + 512], w.indirect(T.o2[:, l0:l0 + 32]), *deps)]
         for sp in range(2):
             for ch in range(2):
                 if any((d, sp + 2 * b) in FAR[ch + 2 * cb] for b in range(2) for cb in range(2)):
-                    m = 32 * a + 16 * sp + 8 * ch + d
-                    last[(a, ch)] = mm(ps[2 * a + ch][:, 0:256], T.wt[:, m::64], T.vv[:, o + sp:o + 512:2],
-                                       (d, sp) == (0, 0), (d, sp) == (7, 1), a_wt, v_wt, *got)
+                    m = 4096 * a + 16 * sp + 8 * ch + d
+                    last[(a, ch)] = mm(ps[2 * a + ch][:, 0:256], T.wt[:, m:4096 * a + 4096:32], T.vv[:, o + sp:o + 512:2],
+                                       (d, sp) == (0, 0), (d, sp) == (7, 1), *(made[a] + got))
 
     def store(a):
         out = [cp("cv" if ch else "ca", T.ysb[:, 512 * a + 256 * ch:512 * a + 256 * ch + 256], ps[2 * a + ch][:, 0:256],
                   last[(a, ch)]) for ch in range(2)]
         dma("sy", T.y[64 * a:64 * a + 64, :], T.ysb[:, 512 * a:512 * a + 512], "dy", *out)
 
+    v_w8.append(weights8(1))
+    made.append([weights(1, "cv", range(8), v_w8[1])])
+    v_o[1, 0] = deal_near(1, 0, t_n[1, 1])
+    v_o[1, 1] = deal_near(1, 1, t_n[1, 3])
     for d in range(8):
         colleagues(0, d)
     for d in range(8):
-        if d == 4:
+        if d == 3:
             store(0)
         colleagues(1, d)
     store(1)

from concourse.mybir import AluOpType, ActivationFunctionType

N = 4
E, PAD, GH = 4096, 16, 1536
R = E + PAD + GH
Q = 768
DX, DY = (-1, 0, 1, -1, 1, -1, 0, 1), (-1, -1, -1, 0, 0, 1, 1, 1)
FAR = [[(d, s) for d in range(8) for s in range(4)
        if max(abs(2 * DX[d] + s % 2 - c % 2), abs(2 * DY[d] + s // 2 - c // 2)) > 1] for c in range(4)]
RELAY = ((1, 0), (1, 1))
W0 = 3
VD = ((0, 5), (0, 7), (1, 1), (1, 3), (1, 5))

SCRATCH = {
    "win": ("sbuf", [128, 2 * R], "bfloat16"),
    "kidw": ("sbuf", [128, 1544], "int32"),
    "giv": ("sbuf", [128, 48], "int32"),
    "nea": ("sbuf", [128, 128], "int32"),
    "gt": ("sbuf", [128, 48], "int32"), "gx": ("sbuf", [128, 48], "int32"),
    "gqu": ("sbuf", [128, 48], "uint16"), "gxu": ("sbuf", [128, 48], "uint16"),
    "nt": ("sbuf", [128, 128], "int32"), "nx": ("sbuf", [128, 128], "int32"),
    "nqu": ("sbuf", [128, 128], "uint16"), "nxu": ("sbuf", [128, 128], "uint16"),
    "pi": ("sbuf", [128, 4], "int32"), "bi": ("sbuf", [128, 8], "int32"), "bf": ("sbuf", [128, 8], "float32"),
    "cf": ("sbuf", [128, 8], "float32"), "cols": ("sbuf", [128, 284], "float32"),
    "sel": ("sbuf", [128, 284], "float32"),
    "rowq": ("sbuf", [128, 8], "float32"),
    "mlo": ("sbuf", [128, 8], "bfloat16"), "mhi": ("sbuf", [128, 8], "bfloat16"), "mhf": ("sbuf", [128, 8], "float32"),
    "ones": ("sbuf", [128, 192], "bfloat16"), "wide": ("sbuf", [128, 192], "bfloat16"),
    "mg": ("sbuf", [128, 768], "float32"), "ag": ("sbuf", [128, 768], "float32"),
    "mn": ("sbuf", [128, 2048], "float32"), "an": ("sbuf", [128, 2048], "float32"),
    "og": ("sbuf", [128, 192], "uint16"), "o2": ("sbuf", [128, 512], "uint16"),
    "gout": ("sbuf", [128, 3072], "bfloat16"),
    "trl": ("sbuf", [128, 108], "bfloat16"), "tall": ("sbuf", [128, 128], "bfloat16"),
    "tst": ("sbuf", [128, 128], "bfloat16"), "w8": ("sbuf", [128, 1024], "bfloat16"),
    "wt": ("sbuf", [128, 8192], "bfloat16"),
    "vv": ("sbuf", [128, 8192], "bfloat16"),
    "ysb": ("sbuf", [128, 1024], "float32"),
}
for _k in range(8):
    SCRATCH["ps%d" % _k] = ("psum", [128, 512], "float32")

SEMAPHORES = ["cv", "ca", "ct", "cg", "dgive", "dkid", "dex0", "dex1", "dnear", "dtr", "dy",
              "arr0", "arr1", "sent", "hop0", "hop1"]


def far_runs():
    runs = []
    for c in range(4):
        for i, (d, s) in enumerate(FAR[c]):
            src, dst = 27 * c + i, 32 * c + 4 * d + s
            if runs and runs[-1][0] + runs[-1][2] == src and runs[-1][1] + runs[-1][2] == dst:
                runs[-1][2] += 1
            else:
                runs.append([src, dst, 1])
    return runs


def way(T, topo, rank, a, dd):
    core, out = T.cores[rank], {}
    if (a, dd) not in RELAY:
        return core, []
    for k in sorted(set(x[1] for x in RELAY)):
        dst = T.cores[(rank + k + 1) % N]
        out[k] = [c for c in topo.cores_of(core) if topo.die(c) != topo.die(core) and c not in T.cores
                  and c not in out.values() and topo.may_write(c, dst)][0]
    dst = T.cores[(rank + dd + 1) % N]
    return out[dd], [e for e in topo.engines(core, out[dd]) if e not in topo.engines(core, dst)]


def hand_on(g, core, T, topo):
    sent = 0
    for rank in range(N):
        for a, dd in RELAY:
            h, hop = way(T, topo, rank, a, dd)
            if h == core:
                dst = T.cores[(rank + dd + 1) % N]
                rid, pid = topo.addr(dst)[0:2]
                o = R * a + E + PAD + 512 * dd
                g.wait_ge(T.sem["hop%d" % a], len(hop))
                g.remote_dma(T.win[:, o:o + 512], T.gout[:, 512 * a:512 * a + 512], T.sem["arr%d" % a], T.sem.sent,
                             pid, rid, topo.mask(core, dst))
                sent += len(topo.engines(core, dst))
    if sent:
        g.wait_ge(T.sem.sent, sent)


def rank_program(g, core, T, topo):
    rank = T.rank_of(core)
    if rank is None:
        hand_on(g, core, T, topo)
        return
    A, F = AluOpType, ActivationFunctionType
    V, S, P, Y = g.vector, g.scalar, g.tensor, g.sync
    queue = {"cv": V, "ca": S, "ct": P, "cg": g, "sy": Y}
    count, seen = {}, {}

    def need(q, deps):
        for sem, n in deps:
            if seen.get((q, sem), 0) < n:
                queue[q].wait_ge(T.sem[sem], n)
                seen[(q, sem)] = n

    def done(ins, sem, n):
        ins.then_inc(T.sem[sem], n)
        count[sem] = count.get(sem, 0) + n
        return (sem, count[sem])

    def ts(out, in0, s1, s2, op0, op1, *deps):
        need("cv", deps)
        return done(V.tensor_scalar(out, in0, s1, s2, op0) if op1 is None else V.tensor_scalar(out, in0, s1, s2, op0, op1), "cv", 1)

    def tt(out, in0, in1, op, *deps):
        need("cv", deps)
        return done(V.tensor_tensor(out, in0, in1, op), "cv", 1)

    def cp(q, out, in_, *deps):
        need(q, deps)
        return done(V.tensor_copy(out, in_) if q == "cv" else S.activation(out, in_, F.Copy), q, 1)

    def mm(out, lhsT, rhs, start, stop, *deps):
        need("ct", deps)
        return done(P.matmul(out, lhsT, rhs, start, stop), "ct", 1)

    def dma(q, out, in_, sem, *deps):
        need(q, deps)
        return done(queue[q].dma_start(out, in_), sem, 16)

    def pool(ins):
        t = done(ins, "cg", 1)
        need("cg", [t])
        return t

    ps = [T["ps%d" % k] for k in range(8)]
    win = T.win

    d_give = dma("sy", T.giv[:], T.give[:], "dgive")
    d_kid = dma("sy", T.kidw[:, 0:Q], T.kid[:], "dkid")
    d_ex = [[dma("sy", win[64 * b:64 * b + 64, R * a:R * a + E], T.ex[64 * a:64 * a + 64, :], "dex%d" % a)
             for b in range(2)][1] for a in range(2)]
    d_tr = dma("ca", T.trl[:], T.tr[:], "dtr")
    d_near = dma("ca", T.nea[:], T.near[:], "dnear")

    g_pi = pool(g.iota(T.pi[:, 0:1], [[0, 1]], 0, 1))
    g_cols = pool(g.iota(T.cols[:], [[1, 284]], -14, 0, allow_small_or_imprecise_dtypes=True))
    pool(g.iota(win[:, E:E + PAD], [[0, PAD]], 0, 0, allow_small_or_imprecise_dtypes=True))
    pool(g.iota(win[:, R + E:R + E + PAD], [[0, PAD]], 0, 0, allow_small_or_imprecise_dtypes=True))
    g_zero = pool(g.iota(T.kidw[:, 2 * Q:2 * Q + 8], [[0, 8]], E, 0))
    pool(g.iota(T.ones[:], [[0, 192]], 1, 0, allow_small_or_imprecise_dtypes=True))
    for b in range(2):
        g_wide = pool(g.affine_select(T.wide[64 * b:64 * b + 64, :], T.ones[64 * b:64 * b + 64, :], [[-1, 192]],
                                      A.is_equal, 0.0, 64, 1))

    v_tz = done(V.memset(T.tall[:], 0.0), "cv", 1)
    pi, bi, bf, cf = T.pi[:, 0:1], T.bi, T.bf, T.cf
    for k, (sh, mask) in enumerate([(0, 48), (3, 1), (2, 1), (6, 1), (0, 3), (0, 7), (3, 7)]):
        t = ts(bi[:, k:k + 1], pi, sh, mask, A.logical_shift_right, A.bitwise_and, g_pi)
    v_bf = cp("cv", bf[:, 0:7], bi[:, 0:7], t)
    k16, cb_, sp_, a_, q_, xlo, xhi = [bf[:, k:k + 1] for k in range(7)]
    t = ts(cf[:, 0:1], cb_, 64.0, k16, A.mult, A.add, v_bf)
    for k in range(3):
        ts(cf[:, 2 + k:3 + k], sp_, float(E + PAD + 512 * k), None, A.add, None)
    v_cf = ts(cf[:, 1:2], a_, 142.0, cf[:, 0:1], A.mult, A.add, t)
    v_rowq = ts(T.rowq[:], T.cols[:, 14:22], 3.0, q_, A.min, A.is_equal, g_cols)
    v_sel = ts(T.sel[:], T.cols[:], sp_, cf[:, 1:2], A.subtract, A.is_equal, v_cf)

    def ghosts(k):
        return ts(T.kidw[:, Q + 256 * k:Q + 256 * k + 256], T.cols[:, 14:270], 2.0, cf[:, 2 + k:3 + k], A.mult, A.add)

    def quarter(n, qu, loaded):
        return ts(qu[:], n[:], -383.6, 1.0 / Q, A.add, A.mult, loaded)

    def place(n, qu, t_, x, xu, have):
        t2 = ts(t_[:], qu[:], 3.0, -float(Q), A.min, A.mult, have)
        t3 = tt(x[:], n[:], t_[:], A.add, t2)
        return cp("cv", xu[:], x[:], t3)

    ghosts(0)
    ghosts(1)
    v_gq = quarter(T.giv, T.gqu, d_give)
    v_ghost = ghosts(2)
    v_gx = place(T.giv, T.gqu, T.gt, T.gx, T.gxu, v_gq)
    v_nq = quarter(T.nea, T.nqu, d_near)

    runs = far_runs()

    def spread(part):
        return [cp("ca", T.tall[:, dst:dst + n], T.trl[:, src:src + n], d_tr, v_tz) for src, dst, n in part][-1]

    spread(runs[:5])

    a_mg = [cp("ca", T.mg[:, 384 * k:384 * k + 384], T.rowq[:].indirect(T.gqu[:, 24 * k:24 * k + 24]), v_rowq, v_gq)
            for k in range(2)]
    v_nx = place(T.nea, T.nqu, T.nt, T.nx, T.nxu, v_nq)
    v_ag = [tt(T.ag[:, 384 * k:384 * k + 384], T.kidw[:, 0:Q].indirect(T.gxu[:, 24 * k:24 * k + 24]),
               T.mg[:, 384 * k:384 * k + 384], A.mult, d_kid, v_gx, a_mg[k]) for k in range(2)]
    t_og = []
    for a in range(2):
        for k0, k1 in ((0, 1), (1, 2)) if a == 0 else ((0, 2),):
            for jj in range(8):
                o = 142 * a + 14 - 2 * jj
                t = mm(ps[4 + a][:, 48 * k0:48 * k1], T.sel[:, o:o + 128], T.ag[:, 384 * k0 + jj:384 * k1:8],
                       jj == 0, jj == 7, v_sel, v_ag[k1 - 1])
        t_og.append(t)

    def mask_near(k):
        return cp("ca", T.mn[:, 512 * k:512 * k + 512], T.rowq[:].indirect(T.nqu[:, 32 * k:32 * k + 32]), v_nq)

    def kids_near(k, m):
        return tt(T.an[:, 512 * k:512 * k + 512], T.kidw[:, 0:1544].indirect(T.nxu[:, 32 * k:32 * k + 32]),
                  T.mn[:, 512 * k:512 * k + 512], A.mult, v_nx, v_ghost, g_zero, m)

    def bank(a, h):
        return ps[6 + a - 2 * h]

    def list_near(a, k, *deps):
        for jj in range(8):
            c = 142 * a + 14 - 2 * jj
            t = mm(bank(a, k // 2)[:, 64 * (k % 2):64 * (k % 2) + 64], T.sel[:, c:c + 128],
                   T.an[:, 512 * k + jj:512 * k + 512:8], jj == 0, jj == 7, *deps)
        return t

    def deal_near(a, h, formed):
        return cp("cv", T.o2[:, 256 * a + 128 * h:256 * a + 128 * h + 128], bank(a, h)[:, 0:128], formed)

    def gather_give(q, a, c0, c1, listed):
        return cp(q, T.gout[:, 1536 * a + 16 * c0:1536 * a + 16 * c1],
                  win[:, R * a:R * a + E + PAD].indirect(T.og[:, 96 * a + c0:96 * a + c1]), listed, d_ex[a], g_zero)

    def send(a, dd, deps):
        need("cg", deps)
        piece = T.gout[:, 1536 * a + 512 * dd:1536 * a + 512 * dd + 512]
        h, hop = way(T, topo, rank, a, dd)
        if hop:
            rid, pid = topo.addr(h)[0:2]
            g.remote_dma(T.gout[:, 512 * a:512 * a + 512], piece, T.sem["hop%d" % a], T.sem.sent, pid, rid,
                         sum(1 << e for e in hop))
        else:
            dst = T.cores[(rank + dd + 1) % N]
            assert topo.may_write(core, dst)
            rid, pid = topo.addr(dst)[0:2]
            o = R * a + E + PAD + 512 * dd
            hop = topo.engines(core, dst)
            g.remote_dma(win[:, o:o + 512], piece, T.sem["arr%d" % a], T.sem.sent, pid, rid, topo.mask(core, dst))
        count["sent"] = count.get("sent", 0) + len(hop)
        writer = way(T, topo, (rank - dd - 1) % N, a, dd)[0]
        count["arr%d" % a] = count.get("arr%d" % a, 0) + len(topo.engines(writer, core))

    a_mn = [mask_near(0), mask_near(1)]
    a_tall = spread(runs[5:])
    t_tst = []
    for a in range(2):
        for cb in range(2):
            for sp in range(2):
                for b in range(2):
                    o = 32 * cb + 16 * sp
                    t = mm(ps[2 * a][:, o:o + 16], T.wide[64 * a:64 * a + 64, 64 - 64 * b:192 - 64 * b],
                           T.tall[64 * a:64 * a + 64, 64 * cb + 2 * b + sp:64 * cb + 64:4], b == 0, b == 1, g_wide, a_tall)
        t_tst.append(t)

    def weights8(a):
        t = cp("cv", T.tst[:, 64 * a:64 * a + 64], ps[2 * a][:, 0:64], t_tst[a])
        return [ts(T.w8[:, 512 * a + 64 * k:512 * a + 64 * k + 64], T.tst[:, 64 * a:64 * a + 64], T.mlo[:, k:k + 1], None,
                   A.mult, None, t) for k in range(8)][-1]

    def weights(a, q, ks, w8):
        need(q, [w8])
        for k in ks:
            out, src = T.wt[:, 4096 * a + 512 * k:4096 * a + 512 * k + 512], T.w8[:, 512 * a:512 * a + 512]
            if q == "ca":
                t = done(S.activation(out, src, F.Copy, scale=T.mhf[:, k:k + 1]), "ca", 1)
            else:
                t = ts(out, src, T.mhi[:, k:k + 1], None, A.mult, None)
        return t

    ts(T.mlo[:], T.cols[:, 14:22], xlo, None, A.is_equal, None)
    ts(T.mhi[:], T.cols[:, 14:22], xhi, None, A.is_equal, None)
    ts(T.mhf[:], T.cols[:, 14:22], xhi, None, A.is_equal, None)
    t_n, v_an = {}, [kids_near(0, a_mn[0])]
    v_og0 = cp("cv", T.og[:, 0:96], ps[4][:, 0:96], t_og[0])
    for dd in range(N - 1):
        send(0, dd, [gather_give("cv", 0, 32 * dd, 32 * dd + 16, v_og0), gather_give("ca", 0, 32 * dd + 16, 32 * dd + 32, v_og0)])
    v_og1 = cp("cv", T.og[:, 96:192], ps[5][:, 0:96], t_og[1])
    a_mn += [mask_near(2), mask_near(3)]
    v_an += [kids_near(1, a_mn[1]), kids_near(2, a_mn[2])]
    for k in range(2):
        t_n[0, k] = list_near(0, k, v_an[k])
        t_n[1, k] = list_near(1, k)
    send(1, 0, [gather_give("ca", 1, 0, 32, v_og1)])
    send(1, 1, [gather_give("cv", 1, 32, 64, v_og1)])
    send(1, 2, [gather_give("ca", 1, 64, 96, v_og1)])
    v_w8 = [weights8(0)]
    v_an.append(kids_near(3, a_mn[3]))
    for k in range(2, 4):
        t_n[0, k] = list_near(0, k, v_an[k], v_og0)
    for k in range(2, 4):
        t_n[1, k] = list_near(1, k, v_og1)
    v_o = {(0, 0): deal_near(0, 0, t_n[0, 1])}
    made = [[weights(0, "ca", range(W0), v_w8[0]), weights(0, "cv", range(W0, 8), v_w8[0])]]
    v_o[0, 1] = deal_near(0, 1, t_n[0, 3])

    last = {}

    def colleagues(a, d):
        o, l0, w = 4096 * a + 512 * d, 256 * a + 32 * d, win[:, R * a:R * a + R]
        deps = [("arr%d" % a, count["arr%d" % a]), v_o[a, d // 4], d_ex[a]]
        if (a, d) == (1, 7):
            got = [cp(q, T.vv[:, o + 256 * k:o + 256 * k + 256], w.indirect(T.o2[:, l0 + 16 * k:l0 + 16 * k + 16]), *deps)
                   for k, q in enumerate(("cv", "ca"))]
        else:
            got = [cp("cv" if (a, d) in VD else "ca", T.vv[:, o:o + 512], w.indirect(T.o2[:, l0:l0 + 32]), *deps)]
        for sp in range(2):
            for ch in range(2):
                if any((d, sp + 2 * b) in FAR[ch + 2 * cb] for b in range(2) for cb in range(2)):
                    m = 4096 * a + 16 * sp + 8 * ch + d
                    last[(a, ch)] = mm(ps[2 * a + ch][:, 0:256], T.wt[:, m:4096 * a + 4096:32], T.vv[:, o + sp:o + 512:2],
                                       (d, sp) == (0, 0), (d, sp) == (7, 1), *(made[a] + got))

    def store(a):
        out = [cp("cv" if ch else "ca", T.ysb[:, 512 * a + 256 * ch:512 * a + 256 * ch + 256], ps[2 * a + ch][:, 0:256],
                  last[(a, ch)]) for ch in range(2)]
        dma("sy", T.y[64 * a:64 * a + 64, :], T.ysb[:, 512 * a:512 * a + 512], "dy", *out)

    v_w8.append(weights8(1))
    made.append([weights(1, "cv", range(8), v_w8[1])])
    v_o[1, 0] = deal_near(1, 0, t_n[1, 1])
    v_o[1, 1] = deal_near(1, 1, t_n[1, 3])
    for d in range(8):
        colleagues(0, d)
    for d in range(8):
        if d == 3:
            store(0)
        colleagues(1, d)
    store(1)

    need("cg", sorted(count.items()))
